import numpy as np
import ml_dtypes


def mxq(x, axis, fmt="e4m3"):
    dtype, down = {"e4m3": (ml_dtypes.float8_e4m3fn, 7), "e5m2": (ml_dtypes.float8_e5m2, 14)}[fmt]
    v = np.moveaxis(np.asarray(x, np.float32).astype(ml_dtypes.bfloat16).astype(np.float64), axis, -1)
    blocks = v.reshape(v.shape[:-1] + (-1, 32))
    amax = np.abs(blocks).max(-1, keepdims=True)
    byte = np.maximum(np.where(amax > 0, np.frexp(amax)[1] - 1 + 127, 0) - down, 1)
    scale = np.exp2(byte - 127.0)
    codes = (blocks / scale).astype(np.float32).astype(dtype).astype(np.float64)
    return np.moveaxis((codes * scale).reshape(v.shape), -1, axis)


WIDE = False


def mx_kscale(k):
    if not WIDE:
        return np.ones(k)
    levels = np.array([10, -10, 5, -5, 0])
    if k % 512:
        return np.exp2(np.random.permutation(np.resize(levels, k // 32))).repeat(32)
    a = np.empty((k // 512, 16))
    for p in range(k // 512):
        a[p, :8] = np.random.permutation(np.resize(levels, 8))
        for g in range(8):
            far = levels[np.abs(levels - a[p, g]) >= 10]
            a[p, g + 8] = far[np.random.randint(len(far))]
    return np.exp2(a.ravel()).repeat(32)


def f64(x):
    return np.asarray(x).astype(np.float64)


def striped(idx):
    return np.tile(idx.reshape(-1, 16).T, (8, 1)).astype(np.uint16)


def unstriped(offs):
    return offs[:16].T.reshape(-1).astype(np.int64)


def striped8(idx):
    return np.concatenate([x.reshape(-1, 16).T for x in idx]).astype(np.uint16)


def runs(offs, k):
    lists = np.stack([offs[16 * r : 16 * r + 16].T.reshape(-1) for r in range(8)]).astype(np.int64)
    return lists[np.arange(k) % 512 // 64]


def pack_weight(w):
    k, n = w.shape
    w = f64(np.asarray(w, np.float32).astype(ml_dtypes.bfloat16)).reshape(k // 32, 32, n)
    amax = np.abs(w).max(1)
    byte = np.clip(np.where(amax > 0, np.frexp(amax)[1] - 1 + 127 - 7, 1), 1, 254)
    scaled = (w * np.exp2(127.0 - byte)[:, None, :]).reshape(k, n).astype(np.float32)
    words = np.ascontiguousarray(scaled.reshape(k // 512, 128, 4, n).transpose(0, 1, 3, 2)).astype(ml_dtypes.float8_e4m3fn).view(np.uint8)
    return words, np.ascontiguousarray(byte.astype(np.uint8).reshape(k // 512, 16, n))


def unpack_weight(words, scales):
    g, p, n, _ = words.shape
    vals = np.ascontiguousarray(words).view(ml_dtypes.float8_e4m3fn).astype(np.float64) * np.repeat(np.exp2(scales.astype(np.float64) - 127.0), 8, axis=1)[..., None]
    return vals.transpose(0, 1, 3, 2).reshape(g * 512, n)


def sigmoid(v):
    return 1.0 / (1.0 + np.exp(-np.maximum(v, -700.0)))

def planes(y):
    n, m = y.shape
    v = y.astype(np.float32).astype(ml_dtypes.bfloat16).astype(np.float64).reshape(n // 32, 32, m)
    top = np.abs(v).max(1)
    byte = np.clip(np.where(top > 0, np.frexp(top)[1] - 1 + 127 - 7, 1), 1, 254)
    codes = (v * np.exp2(127.0 - byte)[:, None, :]).reshape(n, m).astype(np.float32).astype(ml_dtypes.float8_e4m3fn).view(np.uint8)
    words = codes.reshape(n // 512, 128, 4, m).transpose(0, 1, 3, 2)
    return np.ascontiguousarray(words), np.ascontiguousarray(byte.astype(np.uint8).reshape(n // 512, 16, m))


K, T, S, N, H = 512, 2048, 512, 512, 512


def setup_inputs():
    n = np.random.standard_normal
    s = mx_kscale(K)[:, None]
    u = mx_kscale(H)
    packed_xT = pack_weight(n((K, T)) * s)
    packed_w1 = pack_weight(n((K, H)) / np.sqrt(K) / s)
    packed_w2 = pack_weight(n((H, N)) / np.sqrt(H) / u[:, None])
    return {
        "x_words": packed_xT[0],
        "x_scales": packed_xT[1],
        "w1_words": packed_w1[0],
        "w1_scales": packed_w1[1],
        "gn": (np.random.uniform(0.5, 1.5, (H, 1)) * u[:, None]).astype(np.float32),
        "w2_words": packed_w2[0],
        "w2_scales": packed_w2[1],
        "offs": striped(np.random.permutation(T)[:S]),
        "n1": striped8(np.stack([np.random.permutation(S) for _ in range(8)])),
        "n2": striped8(np.stack([np.random.permutation(S) for _ in range(8)])),
        "n3": striped8(np.stack([np.random.permutation(S) for _ in range(8)])),
    }


def reference(x_words, x_scales, w1_words, w1_scales, gn, w2_words, w2_scales, offs, n1, n2, n3):
    xq = unpack_weight(x_words, x_scales)[:, unstriped(offs)]
    y = unpack_weight(w1_words, w1_scales).T @ xq
    z = f64(gn) * (y * (sigmoid(y[np.arange(H)[:, None], runs(n1, H)])))
    h = unpack_weight(w2_words, w2_scales).T @ mxq(z, 0, "e4m3")
    out_0 = 0.75 * ((h - (h[np.arange(N)[:, None], runs(n2, N)])) * (h - (h[np.arange(N)[:, None], runs(n3, N)])))
    return (out_0,) + planes(out_0)

@@ -1,0 +1,210 @@
+from contextlib import ExitStack
+
+import concourse.mybir as mybir
+
+K, T, S, N, H = 512, 2048, 512, 512, 512
+FLOPS = 2 * K * H * S + 2 * H * N * S
+
+F32 = mybir.dt.float32
+BF16 = mybir.dt.bfloat16
+I32 = mybir.dt.int32
+U32 = mybir.dt.uint32
+U16 = mybir.dt.uint16
+U8 = mybir.dt.uint8
+FP8X4 = mybir.dt.float8_e4m3fn_x4
+MULT = mybir.AluOpType.mult
+SUB = mybir.AluOpType.subtract
+SIGMOID = mybir.ActivationFunctionType.Sigmoid
+
+P = 128
+PACK = 4
+LIST_ROWS = 16
+HALF = S // 2
+BLOCKS = ((0, 256), (256, 128), (384, 128))
+W1_ROW = 4
+W2_ROW = 8
+
+
+def words_of(packed):
+    return packed[0].rearrange("p n t -> p (n t)").bitcast(I32)
+
+
+def entries(lists, start, width):
+    return lists[:, start // LIST_ROWS : (start + width) // LIST_ROWS]
+
+
+def load_scales(queues, plane, scales, row):
+    for q in range(4):
+        queues[q].dma_start(
+            out=plane[32 * q + row : 32 * q + row + 4, :].bitcast(I32),
+            in_=scales[0][4 * q : 4 * q + 4, :].bitcast(I32),
+        )
+
+
+def deal(nc, dealt, raw, run):
+    nc.vector.tensor_copy(
+        out=dealt[:].rearrange("p (t c i) -> p c t i", t=PACK, i=run),
+        in_=raw[:].rearrange("p (c i t) -> p c t i", t=PACK, i=run),
+    )
+
+
+def interleave(copy, grouped, planes):
+    copy(
+        out=grouped[:].rearrange("p (c i t) -> p c t i", t=PACK, i=4),
+        in_=planes[:].rearrange("p t (c i) -> p c t i", i=4),
+    )
+
+
+def tile_picked_laygatequad_none_po_kernel(
+    tc, x_words, x_scales, w1_words, w1_scales, gn, w2_words, w2_scales, offs, n1, n2, n3, out_0, out_1, out_2
+):
+    nc = tc.nc
+    with ExitStack() as ctx:
+        lists = ctx.enter_context(tc.tile_pool(name="lists", bufs=1))
+        keep = ctx.enter_context(tc.tile_pool(name="keep", bufs=1))
+        psum = ctx.enter_context(tc.psum_pool(name="psum", bufs=1))
+
+        offs_t = lists.tile([P, S // LIST_ROWS], U16, name="offs_t")
+        n1_t = lists.tile([P, S // LIST_ROWS], U16, name="n1_t")
+        n2_t = lists.tile([P, S // LIST_ROWS], U16, name="n2_t")
+        n3_t = lists.tile([P, S // LIST_ROWS], U16, name="n3_t")
+
+        xw = keep.tile([P, T], I32, name="xw", align_bytes=64)
+        xs = keep.tile([P, T], U8, name="xs", align_bytes=64)
+        w1w = keep.tile([P, H], I32, name="w1w", align_bytes=64)
+        w1s = keep.tile([P, H], U8, name="w1s", align_bytes=64)
+        w2w = keep.tile([P, N], I32, name="w2w", align_bytes=64)
+        w2s = keep.tile([P, N], U8, name="w2s", align_bytes=64)
+        gain = keep.tile([P, PACK], F32, name="gain")
+        warm = keep.tile([P, 2], F32, name="warm")
+
+        nc.vector.memset(xs[:].bitcast(I32), 0)
+        nc.gpsimd.memset(w1s[:].bitcast(I32), 0)
+        nc.vector.memset(w2s[:].bitcast(I32), 0)
+        nc.vector.memset(warm[:, 0:1], 0.0)
+
+        nc.sync.dma_start(offs_t[:], offs)
+        nc.sync.dma_start(out=w1w[:], in_=words_of(w1_words))
+        nc.sync.dma_start(out=xw[:], in_=words_of(x_words))
+        load_scales([nc.scalar] * 4, xs, x_scales, 0)
+        load_scales([nc.gpsimd, nc.scalar, nc.scalar, nc.scalar], w1s, w1_scales, W1_ROW)
+        nc.scalar.activation(warm[:, 1:2], warm[:, 0:1], SIGMOID)
+        nc.sync.dma_start(n1_t[:], n1)
+        nc.gpsimd.dma_start(out=gain[:], in_=gn.rearrange("(p t) o -> p (t o)", t=PACK))
+        nc.sync.dma_start(out=w2w[:], in_=words_of(w2_words))
+        load_scales([nc.sync] * 4, w2s, w2_scales, W2_ROW)
+        nc.sync.dma_start(n2_t[:], n2)
+        nc.sync.dma_start(n3_t[:], n3)
+
+        w1wd = keep.tile([P, H], I32, name="w1wd", align_bytes=64)
+        deal(nc, w1wd, w1w, 4)
+        xs_g = keep.tile([P, S], U8, name="xs_g", align_bytes=64)
+        nc.vector.tensor_copy(xs_g[:], xs[:].indirect(offs_t[:]))
+        w1sd = keep.tile([P, H], U8, name="w1sd", align_bytes=64)
+        deal(nc, w1sd, w1s, 16)
+
+        y = [keep.tile([P, S], F32, name=f"y{t}") for t in range(PACK)]
+        y_ps = {}
+        for half in range(2):
+            cols = slice(half * HALF, (half + 1) * HALF)
+            xw_g = keep.tile([P, HALF], I32, name=f"xw_g{half}", align_bytes=64)
+            nc.vector.tensor_copy(
+                xw_g[:].bitcast(U32), xw[:].bitcast(U32).indirect(entries(offs_t, half * HALF, HALF))
+            )
+            for pair in range(2):
+                bank = psum.tile([P, 2, HALF], F32, name=f"y_ps{half}{pair}")
+                for u in range(2):
+                    t = 2 * pair + u
+                    y_ps[half, t] = bank[:, u, :]
+                    nc.tensor.matmul_mx(
+                        out=bank[:, u, :],
+                        lhsT=w1wd[:, t * P : (t + 1) * P].bitcast(FP8X4),
+                        lhsT_scale=w1sd[W1_ROW:P, t * P : (t + 1) * P],
+                        rhs=xw_g[:].bitcast(FP8X4),
+                        rhs_scale=xs_g[:, cols],
+                        start=True,
+                        stop=True,
+                    )
+        w2wd = keep.tile([P, N], I32, name="w2wd", align_bytes=64)
+        deal(nc, w2wd, w2w, 4)
+        for t in range(PACK):
+            nc.scalar.copy(y[t][:, 0:HALF], y_ps[0, t])
+            nc.vector.tensor_copy(y[t][:, HALF:S], y_ps[1, t])
+        w2sd = keep.tile([P, N], U8, name="w2sd", align_bytes=64)
+        deal(nc, w2sd, w2s, 16)
+
+        h_ps = {}
+        for b, (c0, w) in enumerate(BLOCKS):
+            z_planes = keep.tile([P, PACK, w], BF16, name=f"z_planes{b}", align_bytes=64)
+            for t in range(PACK):
+                gate = keep.tile([P, w], F32, name=f"gate{b}{t}")
+                nc.scalar.activation(gate[:], y[t][:].indirect(entries(n1_t, c0, w)), SIGMOID)
+                nc.vector.scalar_tensor_tensor(
+                    z_planes[:, t, :], y[t][:, c0 : c0 + w], gain[:, t : t + 1], gate[:], MULT, MULT
+                )
+            z = keep.tile([P, PACK * w], BF16, name=f"z{b}", align_bytes=64)
+            interleave(nc.vector.tensor_copy, z, z_planes)
+            zw = keep.tile([P, w], I32, name=f"zw{b}", align_bytes=64)
+            zs = keep.tile([P, w], U8, name=f"zs{b}", align_bytes=64)
+            nc.vector.quantize_mx(out=zw[:].bitcast(FP8X4), scales=zs[:], in_=z[:])
+            per_bank = 512 // w
+            for g in range(PACK // per_bank):
+                bank = psum.tile([P, per_bank, w], F32, name=f"h_ps{b}{g}")
+                h_ps[b, g] = bank
+                for u in range(per_bank):
+                    t = per_bank * g + u
+                    nc.tensor.matmul_mx(
+                        out=bank[:, u, :],
+                        lhsT=w2wd[:, t * P : (t + 1) * P].bitcast(FP8X4),
+                        lhsT_scale=w2sd[W2_ROW:P, t * P : (t + 1) * P],
+                        rhs=zw[:].bitcast(FP8X4),
+                        rhs_scale=zs[:],
+                        start=True,
+                        stop=True,
+                    )
+
+        h = [keep.tile([P, S], F32, name=f"h{t}") for t in range(PACK)]
+        own = {}
+        for t in range(PACK):
+            for b, (c0, w) in enumerate(BLOCKS):
+                per_bank = 512 // w
+                g, u = divmod(t, per_bank)
+                nc.scalar.copy(h[t][:, c0 : c0 + w], h_ps[b, g][:, u, :])
+                if b == 0:
+                    own[b, t] = keep.tile([P, w], F32, name=f"own{b}{t}")[:]
+                    nc.scalar.copy(own[b, t], h_ps[b, g][:, u, :])
+        for b, (c0, w) in enumerate(BLOCKS):
+            if b > 0:
+                both = keep.tile([P, PACK, w], F32, name=f"own{b}")
+                nc.scalar.copy(both[:], h_ps[b, 0][:])
+                for t in range(PACK):
+                    own[b, t] = both[:, t, :]
+
+        out_rows = out_0.rearrange("(p t) s -> p t s", t=PACK)
+        out_words = words_of(out_1)
+        ow = keep.tile([P, S], I32, name="ow", align_bytes=64)
+        osc = keep.tile([P, S], U8, name="osc", align_bytes=64)
+        for b, (c0, w) in enumerate(BLOCKS):
+            res = keep.tile([P, PACK, w], F32, name=f"res{b}")
+            diffs = []
+            for t in range(PACK + 1):
+                if t < PACK:
+                    d2 = keep.tile([P, w], F32, name=f"d2_{b}{t}")
+                    d3 = keep.tile([P, w], F32, name=f"d3_{b}{t}")
+                    nc.vector.tensor_tensor(d2[:], h[t][:].indirect(entries(n2_t, c0, w)), own[b, t], SUB)
+                    nc.vector.tensor_tensor(d3[:], h[t][:].indirect(entries(n3_t, c0, w)), own[b, t], SUB)
+                    diffs.append((d2, d3))
+                if t > 0:
+                    d2, d3 = diffs[t - 1]
+                    nc.vector.scalar_tensor_tensor(res[:, t - 1, :], d2[:], 0.75, d3[:], MULT, MULT)
+            nc.sync.dma_start(out=out_rows[:, :, c0 : c0 + w], in_=res[:])
+            grouped = keep.tile([P, PACK * w], BF16, name=f"grouped{b}", align_bytes=64)
+            last = b == len(BLOCKS) - 1
+            interleave(nc.vector.tensor_copy if last else nc.scalar.copy, grouped, res)
+            nc.vector.quantize_mx(out=ow[:, c0 : c0 + w].bitcast(FP8X4), scales=osc[:, c0 : c0 + w], in_=grouped[:])
+            nc.sync.dma_start(out=out_words[:, c0 : c0 + w], in_=ow[:, c0 : c0 + w])
+        for q in range(4):
+            queue = nc.scalar if q % 2 else nc.sync
+            queue.dma_start(
+                out=out_2[0][4 * q : 4 * q + 4, :].bitcast(I32), in_=osc[32 * q : 32 * q + 4, :].bitcast(I32)
+            )

@@ -15,12 +15,14 @@ FP8X4 = mybir.dt.float8_e4m3fn_x4
 MULT = mybir.AluOpType.mult
 SUB = mybir.AluOpType.subtract
 SIGMOID = mybir.ActivationFunctionType.Sigmoid
+COPY = mybir.ActivationFunctionType.Copy
 
 P = 128
 PACK = 4
 LIST_ROWS = 16
 HALF = S // 2
 BLOCKS = ((0, 256), (256, 128), (384, 128))
+BANK_TILES = (((0, 2), (2, 4)), ((0, 4),), ((0, 1), (1, 4)))
 W1_ROW = 4
 W2_ROW = 8
 
@@ -51,7 +53,7 @@ def deal(nc, dealt, raw, run):
 def interleave(copy, grouped, planes):
     copy(
         out=grouped[:].rearrange("p (c i t) -> p c t i", t=PACK, i=4),
-        in_=planes[:].rearrange("p t (c i) -> p c t i", i=4),
+        in_=planes.rearrange("p t (c i) -> p c t i", i=4),
     )
 
 
@@ -70,27 +72,28 @@ def tile_picked_laygatequad_none_po_kernel(
         n3_t = lists.tile([P, S // LIST_ROWS], U16, name="n3_t")
 
         xw = keep.tile([P, T], I32, name="xw", align_bytes=64)
-        xs = keep.tile([P, T], U8, name="xs", align_bytes=64)
+        xs = keep.tile([P, T], U8, name="xs", tag="xs", align_bytes=64)
         w1w = keep.tile([P, H], I32, name="w1w", align_bytes=64)
         w1s = keep.tile([P, H], U8, name="w1s", align_bytes=64)
-        w2w = keep.tile([P, N], I32, name="w2w", align_bytes=64)
-        w2s = keep.tile([P, N], U8, name="w2s", align_bytes=64)
+        w2w = keep.tile([P, N], I32, name="w2w", tag="w2w", align_bytes=64)
+        w2s = keep.tile([P, N], U8, name="w2s", tag="w2s", align_bytes=64)
         gain = keep.tile([P, PACK], F32, name="gain")
         warm = keep.tile([P, 2], F32, name="warm")
 
-        nc.vector.memset(xs[:].bitcast(I32), 0)
-        nc.gpsimd.memset(w1s[:].bitcast(I32), 0)
-        nc.vector.memset(w2s[:].bitcast(I32), 0)
+        nc.gpsimd.memset(xs[:].bitcast(I32)[:, 0:256], 0)
         nc.vector.memset(warm[:, 0:1], 0.0)
+        nc.vector.memset(xs[:].bitcast(I32)[:, 256:512], 0)
+        nc.gpsimd.memset(w1s[:].bitcast(I32), 0)
+        nc.scalar.activation(warm[:, 1:2], warm[:, 0:1], SIGMOID)
+        nc.vector.memset(w2s[:].bitcast(I32), 0)
 
         nc.sync.dma_start(offs_t[:], offs)
         nc.sync.dma_start(out=w1w[:], in_=words_of(w1_words))
-        nc.sync.dma_start(out=xw[:], in_=words_of(x_words))
-        load_scales([nc.scalar] * 4, xs, x_scales, 0)
-        load_scales([nc.gpsimd, nc.scalar, nc.scalar, nc.scalar], w1s, w1_scales, W1_ROW)
-        nc.scalar.activation(warm[:, 1:2], warm[:, 0:1], SIGMOID)
         nc.sync.dma_start(n1_t[:], n1)
-        nc.gpsimd.dma_start(out=gain[:], in_=gn.rearrange("(p t) o -> p (t o)", t=PACK))
+        load_scales([nc.sync] * 4, xs, x_scales, 0)
+        nc.sync.dma_start(out=xw[:], in_=words_of(x_words))
+        load_scales([nc.gpsimd, nc.gpsimd, nc.scalar, nc.scalar], w1s, w1_scales, W1_ROW)
+        nc.sync.dma_start(out=gain[:], in_=gn.rearrange("(p t) o -> p (t o)", t=PACK))
         nc.sync.dma_start(out=w2w[:], in_=words_of(w2_words))
         load_scales([nc.sync] * 4, w2s, w2_scales, W2_ROW)
         nc.sync.dma_start(n2_t[:], n2)
@@ -100,59 +103,92 @@ def tile_picked_laygatequad_none_po_kernel(
         deal(nc, w1wd, w1w, 4)
         xs_g = keep.tile([P, S], U8, name="xs_g", align_bytes=64)
         nc.vector.tensor_copy(xs_g[:], xs[:].indirect(offs_t[:]))
-        w1sd = keep.tile([P, H], U8, name="w1sd", align_bytes=64)
+        w1sd = keep.tile([P, H], U8, name="w1sd", tag="xs", align_bytes=64)
         deal(nc, w1sd, w1s, 16)
 
-        y = [keep.tile([P, S], F32, name=f"y{t}") for t in range(PACK)]
+        halves = [slice(0, HALF), slice(HALF, S)]
+        xw_g = keep.tile([P, S], I32, name="xw_g", align_bytes=64)
+        for half in range(2):
+            nc.vector.tensor_copy(
+                xw_g[:, halves[half]].bitcast(U32), xw[:].bitcast(U32).indirect(entries(offs_t, half * HALF, HALF))
+            )
+
+        def project(t, cols, tag):
+            bank = psum.tile([P, cols.stop - cols.start], F32, name=tag, tag=tag)
+            nc.tensor.matmul_mx(
+                out=bank[:],
+                lhsT=w1wd[:, t * P : (t + 1) * P].bitcast(FP8X4),
+                lhsT_scale=w1sd[W1_ROW:P, t * P : (t + 1) * P],
+                rhs=xw_g[:, cols].bitcast(FP8X4),
+                rhs_scale=xs_g[:, cols],
+                start=True,
+                stop=True,
+            )
+            return bank
+
         y_ps = {}
         for half in range(2):
-            cols = slice(half * HALF, (half + 1) * HALF)
-            xw_g = keep.tile([P, HALF], I32, name=f"xw_g{half}", align_bytes=64)
-            nc.vector.tensor_copy(
-                xw_g[:].bitcast(U32), xw[:].bitcast(U32).indirect(entries(offs_t, half * HALF, HALF))
-            )
-            for pair in range(2):
-                bank = psum.tile([P, 2, HALF], F32, name=f"y_ps{half}{pair}")
-                for u in range(2):
-                    t = 2 * pair + u
-                    y_ps[half, t] = bank[:, u, :]
-                    nc.tensor.matmul_mx(
-                        out=bank[:, u, :],
-                        lhsT=w1wd[:, t * P : (t + 1) * P].bitcast(FP8X4),
-                        lhsT_scale=w1sd[W1_ROW:P, t * P : (t + 1) * P],
-                        rhs=xw_g[:].bitcast(FP8X4),
-                        rhs_scale=xs_g[:, cols],
-                        start=True,
-                        stop=True,
-                    )
+            for t in (0, 1):
+                y_ps[half, t] = project(t, halves[half], f"bank{2 * half + t}")
+        for t in (2, 3):
+            y_ps[t] = project(t, slice(0, S), f"bank{2 + t}")
+
+        h = [keep.tile([P, 2 * S if t in (1, 2) else S], F32, name=f"h{t}") for t in range(PACK)]
+        y = [keep.tile([P, S], F32, name=f"y{t}") for t in range(PACK)]
+        gate3 = keep.tile([P, S], F32, name="gate3")
+        gate = {2: h[2][:, S : 2 * S], 3: gate3[:]}
+
         w2wd = keep.tile([P, N], I32, name="w2wd", align_bytes=64)
         deal(nc, w2wd, w2w, 4)
-        for t in range(PACK):
-            nc.scalar.copy(y[t][:, 0:HALF], y_ps[0, t])
-            nc.vector.tensor_copy(y[t][:, HALF:S], y_ps[1, t])
         w2sd = keep.tile([P, N], U8, name="w2sd", align_bytes=64)
         deal(nc, w2sd, w2s, 16)
+        scaled0 = keep.tile([P, S], F32, name="scaled0", tag="w2w", align_bytes=64)
+        scaled = {0: scaled0[:], 1: h[1][:, S : 2 * S]}
+        z_planes = [
+            keep.tile([P, PACK, HALF], F32, name="z_planes0", tag="w2s", align_bytes=64),
+            keep.tile([P, PACK, HALF], F32, name="z_planes1"),
+        ]
+
+        for half in range(2):
+            for t in (0, 1):
+                nc.scalar.activation(y[t][:, halves[half]], y_ps[half, t][:], SIGMOID)
+            nc.vector.tensor_scalar(scaled[0][:, halves[half]], y_ps[half, 0][:], gain[:, 0:1], None, MULT)
+        for half in range(2):
+            nc.scalar.activation(scaled[1][:, halves[half]], y_ps[half, 1][:], COPY, scale=gain[:, 1:2])
+        for t in (0, 1):
+            for half in range(2):
+                nc.vector.tensor_tensor(
+                    z_planes[half][:, t, :],
+                    y[t][:].indirect(entries(n1_t, half * HALF, HALF)),
+                    scaled[t][:, halves[half]],
+                    MULT,
+                )
 
         h_ps = {}
-        for b, (c0, w) in enumerate(BLOCKS):
-            z_planes = keep.tile([P, PACK, w], BF16, name=f"z_planes{b}", align_bytes=64)
-            for t in range(PACK):
-                gate = keep.tile([P, w], F32, name=f"gate{b}{t}")
-                nc.scalar.activation(gate[:], y[t][:].indirect(entries(n1_t, c0, w)), SIGMOID)
-                nc.vector.scalar_tensor_tensor(
-                    z_planes[:, t, :], y[t][:, c0 : c0 + w], gain[:, t : t + 1], gate[:], MULT, MULT
-                )
-            z = keep.tile([P, PACK * w], BF16, name=f"z{b}", align_bytes=64)
-            interleave(nc.vector.tensor_copy, z, z_planes)
+        z = [keep.tile([P, PACK * w], BF16, name=f"z{b}", align_bytes=64) for b, (c0, w) in enumerate(BLOCKS)]
+
+        def planes_of(b):
+            c0, w = BLOCKS[b]
+            return z_planes[c0 // HALF][:, :, c0 % HALF : c0 % HALF + w]
+
+        def gated(t, b):
+            c0, w = BLOCKS[b]
+            nc.scalar.activation(gate[t][:, c0 : c0 + w], y[t][:].indirect(entries(n1_t, c0, w)), SIGMOID)
+            nc.vector.scalar_tensor_tensor(
+                planes_of(b)[:, t, :], y[t][:, c0 : c0 + w], gain[:, t : t + 1], gate[t][:, c0 : c0 + w], MULT, MULT
+            )
+
+        def second_product(b):
+            c0, w = BLOCKS[b]
             zw = keep.tile([P, w], I32, name=f"zw{b}", align_bytes=64)
             zs = keep.tile([P, w], U8, name=f"zs{b}", align_bytes=64)
-            nc.vector.quantize_mx(out=zw[:].bitcast(FP8X4), scales=zs[:], in_=z[:])
-            per_bank = 512 // w
-            for g in range(PACK // per_bank):
-                bank = psum.tile([P, per_bank, w], F32, name=f"h_ps{b}{g}")
+            nc.vector.quantize_mx(out=zw[:].bitcast(FP8X4), scales=zs[:], in_=z[b][:])
+            for g, (t0, t1) in enumerate(BANK_TILES[b]):
+                tag = f"bank{(6 + len(h_ps)) % 8}"
+                bank = psum.tile([P, t1 - t0, w], F32, name=tag, tag=tag)
                 h_ps[b, g] = bank
-                for u in range(per_bank):
-                    t = per_bank * g + u
+                for t in range(t0, t1):
+                    u = t - t0
                     nc.tensor.matmul_mx(
                         out=bank[:, u, :],
                         lhsT=w2wd[:, t * P : (t + 1) * P].bitcast(FP8X4),
@@ -163,48 +199,102 @@ def tile_picked_laygatequad_none_po_kernel(
                         stop=True,
                     )
 
-        h = [keep.tile([P, S], F32, name=f"h{t}") for t in range(PACK)]
-        own = {}
-        for t in range(PACK):
-            for b, (c0, w) in enumerate(BLOCKS):
-                per_bank = 512 // w
-                g, u = divmod(t, per_bank)
-                nc.scalar.copy(h[t][:, c0 : c0 + w], h_ps[b, g][:, u, :])
-                if b == 0:
-                    own[b, t] = keep.tile([P, w], F32, name=f"own{b}{t}")[:]
-                    nc.scalar.copy(own[b, t], h_ps[b, g][:, u, :])
-        for b, (c0, w) in enumerate(BLOCKS):
-            if b > 0:
-                both = keep.tile([P, PACK, w], F32, name=f"own{b}")
-                nc.scalar.copy(both[:], h_ps[b, 0][:])
-                for t in range(PACK):
-                    own[b, t] = both[:, t, :]
+        for t in (2, 3):
+            nc.scalar.copy(y[t][:], y_ps[t][:])
+            gated(t, 0)
+        gated(2, 1)
+        interleave(nc.vector.tensor_copy, z[0], planes_of(0))
+        gated(3, 1)
+        second_product(0)
+        gated(2, 2)
+        gated(3, 2)
+        interleave(nc.scalar.copy, z[1], planes_of(1))
+        second_product(1)
+        interleave(nc.vector.tensor_copy, z[2], planes_of(2))
+        second_product(2)
+
+        own = keep.tile([P, PACK, S], F32, name="own")
+
+        def fill_window(t, b, copy):
+            c0, w = BLOCKS[b]
+            g = 0 if t < BANK_TILES[b][0][1] else 1
+            copy(h[t][:, c0 : c0 + w], h_ps[b, g][:, t - BANK_TILES[b][g][0], :])
+
+        def fill_own(b, g):
+            c0, w = BLOCKS[b]
+            t0, t1 = BANK_TILES[b][g]
+            nc.scalar.copy(own[:, t0:t1, c0 : c0 + w], h_ps[b, g][:])
+
+        fill_window(0, 0, nc.scalar.copy)
+        fill_window(0, 1, nc.scalar.copy)
+        fill_own(0, 0)
+        fill_window(0, 2, nc.vector.tensor_copy)
+        fill_own(1, 0)
+        fill_own(2, 0)
+        fill_own(2, 1)
+        for t in range(1, PACK):
+            for b in range(len(BLOCKS)):
+                fill_window(t, b, nc.scalar.copy)
+            if t == 1:
+                fill_own(0, 1)
 
         out_rows = out_0.rearrange("(p t) s -> p t s", t=PACK)
         out_words = words_of(out_1)
         ow = keep.tile([P, S], I32, name="ow", align_bytes=64)
         osc = keep.tile([P, S], U8, name="osc", align_bytes=64)
+        res = keep.tile([P, PACK, S], F32, name="res")
+        d2 = [keep.tile([P, S], F32, name=f"d2_{t}") for t in range(PACK)]
+        d3 = [keep.tile([P, S], F32, name=f"d3_{t}") for t in range(PACK)]
+        grouped = [keep.tile([P, PACK * w], BF16, name=f"grouped{b}", align_bytes=64) for b, (c0, w) in enumerate(BLOCKS)]
+
+        def differ(d, lists, t, c0, w):
+            nc.vector.tensor_tensor(
+                d[t][:, c0 : c0 + w], h[t][:].indirect(entries(lists, c0, w)), own[:, t, c0 : c0 + w], SUB
+            )
+
+        def product(t, c0, w):
+            cols = slice(c0, c0 + w)
+            nc.vector.scalar_tensor_tensor(res[:, t, cols], d2[t][:, cols], 0.75, d3[t][:, cols], MULT, MULT)
+
+        def store(t, c0, w):
+            nc.sync.dma_start(out=out_rows[:, t, c0 : c0 + w], in_=res[:, t, c0 : c0 + w])
+
+        def regroup(copy, b):
+            c0, w = BLOCKS[b]
+            interleave(copy, grouped[b], res[:, :, c0 : c0 + w])
+
+        def quantise(b):
+            c0, w = BLOCKS[b]
+            nc.vector.quantize_mx(out=ow[:, c0 : c0 + w].bitcast(FP8X4), scales=osc[:, c0 : c0 + w], in_=grouped[b][:])
+
+        for c0 in (0, HALF):
+            differ(d2, n2_t, 0, c0, HALF)
+            differ(d3, n3_t, 0, c0, HALF)
+        for t in (1, 2):
+            differ(d2, n2_t, t, 0, S)
+            product(t - 1, 0, S)
+            store(t - 1, 0, S)
+            differ(d3, n3_t, t, 0, S)
         for b, (c0, w) in enumerate(BLOCKS):
-            res = keep.tile([P, PACK, w], F32, name=f"res{b}")
-            diffs = []
-            for t in range(PACK + 1):
-                if t < PACK:
-                    d2 = keep.tile([P, w], F32, name=f"d2_{b}{t}")
-                    d3 = keep.tile([P, w], F32, name=f"d3_{b}{t}")
-                    nc.vector.tensor_tensor(d2[:], h[t][:].indirect(entries(n2_t, c0, w)), own[b, t], SUB)
-                    nc.vector.tensor_tensor(d3[:], h[t][:].indirect(entries(n3_t, c0, w)), own[b, t], SUB)
-                    diffs.append((d2, d3))
-                if t > 0:
-                    d2, d3 = diffs[t - 1]
-                    nc.vector.scalar_tensor_tensor(res[:, t - 1, :], d2[:], 0.75, d3[:], MULT, MULT)
-            nc.sync.dma_start(out=out_rows[:, :, c0 : c0 + w], in_=res[:])
-            grouped = keep.tile([P, PACK * w], BF16, name=f"grouped{b}", align_bytes=64)
-            last = b == len(BLOCKS) - 1
-            interleave(nc.vector.tensor_copy if last else nc.scalar.copy, grouped, res)
-            nc.vector.quantize_mx(out=ow[:, c0 : c0 + w].bitcast(FP8X4), scales=osc[:, c0 : c0 + w], in_=grouped[:])
-            nc.sync.dma_start(out=out_words[:, c0 : c0 + w], in_=ow[:, c0 : c0 + w])
+            differ(d2, n2_t, 3, c0, w)
+            if b == 0:
+                product(2, 0, S)
+                store(2, 0, S)
+            else:
+                product(3, *BLOCKS[b - 1])
+                regroup(nc.scalar.copy, b - 1)
+            differ(d3, n3_t, 3, c0, w)
+        store(3, 0, HALF)
+        quantise(0)
+        nc.sync.dma_start(out=out_words[:, halves[0]], in_=ow[:, halves[0]])
+        product(3, *BLOCKS[2])
+        store(3, HALF, HALF)
+        regroup(nc.vector.tensor_copy, 2)
+        quantise(1)
+        quantise(2)
+        nc.sync.dma_start(out=out_words[:, halves[1]], in_=ow[:, halves[1]])
         for q in range(4):
-            queue = nc.scalar if q % 2 else nc.sync
+            queue = nc.sync if q % 2 else nc.scalar
             queue.dma_start(
                 out=out_2[0][4 * q : 4 * q + 4, :].bitcast(I32), in_=osc[32 * q : 32 * q + 4, :].bitcast(I32)
             )

@@ -22,7 +22,6 @@ PACK = 4
 LIST_ROWS = 16
 HALF = S // 2
 BLOCKS = ((0, 256), (256, 128), (384, 128))
-BANK_TILES = (((0, 2), (2, 4)), ((0, 4),), ((0, 1), (1, 4)))
 W1_ROW = 4
 W2_ROW = 8
 
@@ -78,22 +77,19 @@ def tile_picked_laygatequad_none_po_kernel(
         w2w = keep.tile([P, N], I32, name="w2w", tag="w2w", align_bytes=64)
         w2s = keep.tile([P, N], U8, name="w2s", tag="w2s", align_bytes=64)
         gain = keep.tile([P, PACK], F32, name="gain")
-        warm = keep.tile([P, 2], F32, name="warm")
 
-        nc.gpsimd.memset(xs[:].bitcast(I32)[:, 0:256], 0)
-        nc.vector.memset(warm[:, 0:1], 0.0)
-        nc.vector.memset(xs[:].bitcast(I32)[:, 256:512], 0)
         nc.gpsimd.memset(w1s[:].bitcast(I32), 0)
-        nc.scalar.activation(warm[:, 1:2], warm[:, 0:1], SIGMOID)
+        nc.gpsimd.memset(xs[:].bitcast(I32)[:, 0:256], 0)
+        nc.vector.memset(xs[:].bitcast(I32)[:, 256:512], 0)
         nc.vector.memset(w2s[:].bitcast(I32), 0)
 
         nc.sync.dma_start(offs_t[:], offs)
         nc.sync.dma_start(out=w1w[:], in_=words_of(w1_words))
-        nc.sync.dma_start(n1_t[:], n1)
+        load_scales([nc.sync, nc.gpsimd, nc.gpsimd, nc.gpsimd], w1s, w1_scales, W1_ROW)
         load_scales([nc.sync] * 4, xs, x_scales, 0)
         nc.sync.dma_start(out=xw[:], in_=words_of(x_words))
-        load_scales([nc.gpsimd, nc.gpsimd, nc.scalar, nc.scalar], w1s, w1_scales, W1_ROW)
         nc.sync.dma_start(out=gain[:], in_=gn.rearrange("(p t) o -> p (t o)", t=PACK))
+        nc.sync.dma_start(n1_t[:], n1)
         nc.sync.dma_start(out=w2w[:], in_=words_of(w2_words))
         load_scales([nc.sync] * 4, w2s, w2_scales, W2_ROW)
         nc.sync.dma_start(n2_t[:], n2)
@@ -114,9 +110,9 @@ def tile_picked_laygatequad_none_po_kernel(
             )
 
         def project(t, cols, tag):
-            bank = psum.tile([P, cols.stop - cols.start], F32, name=tag, tag=tag)
+            out = psum.tile([P, cols.stop - cols.start], F32, name=tag, tag=tag)
             nc.tensor.matmul_mx(
-                out=bank[:],
+                out=out[:],
                 lhsT=w1wd[:, t * P : (t + 1) * P].bitcast(FP8X4),
                 lhsT_scale=w1sd[W1_ROW:P, t * P : (t + 1) * P],
                 rhs=xw_g[:, cols].bitcast(FP8X4),
@@ -124,7 +120,7 @@ def tile_picked_laygatequad_none_po_kernel(
                 start=True,
                 stop=True,
             )
-            return bank
+            return out
 
         y_ps = {}
         for half in range(2):
@@ -133,35 +129,29 @@ def tile_picked_laygatequad_none_po_kernel(
         for t in (2, 3):
             y_ps[t] = project(t, slice(0, S), f"bank{2 + t}")
 
-        h = [keep.tile([P, 2 * S if t in (1, 2) else S], F32, name=f"h{t}") for t in range(PACK)]
+        h = [keep.tile([P, 2 * S if t == 1 else S], F32, name=f"h{t}") for t in range(PACK)]
         y = [keep.tile([P, S], F32, name=f"y{t}") for t in range(PACK)]
-        gate3 = keep.tile([P, S], F32, name="gate3")
-        gate = {2: h[2][:, S : 2 * S], 3: gate3[:]}
+        gate = {t: keep.tile([P, S], F32, name=f"gate{t}") for t in (2, 3)}
 
-        w2wd = keep.tile([P, N], I32, name="w2wd", align_bytes=64)
-        deal(nc, w2wd, w2w, 4)
         w2sd = keep.tile([P, N], U8, name="w2sd", align_bytes=64)
         deal(nc, w2sd, w2s, 16)
-        scaled0 = keep.tile([P, S], F32, name="scaled0", tag="w2w", align_bytes=64)
-        scaled = {0: scaled0[:], 1: h[1][:, S : 2 * S]}
-        z_planes = [
-            keep.tile([P, PACK, HALF], F32, name="z_planes0", tag="w2s", align_bytes=64),
-            keep.tile([P, PACK, HALF], F32, name="z_planes1"),
-        ]
+        w2wd = keep.tile([P, N], I32, name="w2wd", tag="w2s", align_bytes=64)
+        deal(nc, w2wd, w2w, 4)
+        work = keep.tile([P, 2 * PACK + 2, HALF], F32, name="work", tag="w2w", align_bytes=64)
+        z_planes = [work[:, PACK * half : PACK * (half + 1), :] for half in range(2)]
+        scaled = [[work[:, 2 * PACK + half, :] for half in range(2)], [h[1][:, S : S + HALF], h[1][:, S + HALF : 2 * S]]]
 
         for half in range(2):
             for t in (0, 1):
                 nc.scalar.activation(y[t][:, halves[half]], y_ps[half, t][:], SIGMOID)
-            nc.vector.tensor_scalar(scaled[0][:, halves[half]], y_ps[half, 0][:], gain[:, 0:1], None, MULT)
         for half in range(2):
-            nc.scalar.activation(scaled[1][:, halves[half]], y_ps[half, 1][:], COPY, scale=gain[:, 1:2])
+            nc.scalar.activation(scaled[1][half], y_ps[half, 1][:], COPY, scale=gain[:, 1:2])
         for t in (0, 1):
             for half in range(2):
+                if t == 0:
+                    nc.vector.tensor_scalar(scaled[0][half], y_ps[half, 0][:], gain[:, 0:1], None, MULT)
                 nc.vector.tensor_tensor(
-                    z_planes[half][:, t, :],
-                    y[t][:].indirect(entries(n1_t, half * HALF, HALF)),
-                    scaled[t][:, halves[half]],
-                    MULT,
+                    z_planes[half][:, t, :], y[t][:].indirect(entries(n1_t, half * HALF, HALF)), scaled[t][half], MULT
                 )
 
         h_ps = {}
@@ -178,26 +168,36 @@ def tile_picked_laygatequad_none_po_kernel(
                 planes_of(b)[:, t, :], y[t][:, c0 : c0 + w], gain[:, t : t + 1], gate[t][:, c0 : c0 + w], MULT, MULT
             )
 
-        def second_product(b):
+        zw = [keep.tile([P, w], I32, name=f"zw{b}", align_bytes=64) for b, (c0, w) in enumerate(BLOCKS)]
+        zs = [keep.tile([P, w], U8, name=f"zs{b}", align_bytes=64) for b, (c0, w) in enumerate(BLOCKS)]
+
+        def quantise_z(b):
+            nc.vector.quantize_mx(out=zw[b][:].bitcast(FP8X4), scales=zs[b][:], in_=z[b][:])
+
+        def second_product(b, t, out):
+            h_ps[b, t] = out
+            nc.tensor.matmul_mx(
+                out=out,
+                lhsT=w2wd[:, t * P : (t + 1) * P].bitcast(FP8X4),
+                lhsT_scale=w2sd[W2_ROW:P, t * P : (t + 1) * P],
+                rhs=zw[b][:].bitcast(FP8X4),
+                rhs_scale=zs[b][:],
+                start=True,
+                stop=True,
+            )
+
+        def bank(number, tiles, width):
+            return psum.tile([P, tiles, width], F32, name=f"bank{number}", tag=f"bank{number}")
+
+        own = keep.tile([P, PACK, S], F32, name="own")
+
+        def fill_window(t, b, copy):
             c0, w = BLOCKS[b]
-            zw = keep.tile([P, w], I32, name=f"zw{b}", align_bytes=64)
-            zs = keep.tile([P, w], U8, name=f"zs{b}", align_bytes=64)
-            nc.vector.quantize_mx(out=zw[:].bitcast(FP8X4), scales=zs[:], in_=z[b][:])
-            for g, (t0, t1) in enumerate(BANK_TILES[b]):
-                tag = f"bank{(6 + len(h_ps)) % 8}"
-                bank = psum.tile([P, t1 - t0, w], F32, name=tag, tag=tag)
-                h_ps[b, g] = bank
-                for t in range(t0, t1):
-                    u = t - t0
-                    nc.tensor.matmul_mx(
-                        out=bank[:, u, :],
-                        lhsT=w2wd[:, t * P : (t + 1) * P].bitcast(FP8X4),
-                        lhsT_scale=w2sd[W2_ROW:P, t * P : (t + 1) * P],
-                        rhs=zw[:].bitcast(FP8X4),
-                        rhs_scale=zs[:],
-                        start=True,
-                        stop=True,
-                    )
+            copy(h[t][:, c0 : c0 + w], h_ps[b, t])
+
+        def fill_own(b, t0, t1, source):
+            c0, w = BLOCKS[b]
+            nc.scalar.copy(own[:, t0:t1, c0 : c0 + w], source)
 
         for t in (2, 3):
             nc.scalar.copy(y[t][:], y_ps[t][:])
@@ -205,38 +205,42 @@ def tile_picked_laygatequad_none_po_kernel(
         gated(2, 1)
         interleave(nc.vector.tensor_copy, z[0], planes_of(0))
         gated(3, 1)
-        second_product(0)
+        quantise_z(0)
+        for t in (0, 1):
+            second_product(0, t, bank(6 + t, 1, HALF)[:, 0, :])
         gated(2, 2)
         gated(3, 2)
         interleave(nc.scalar.copy, z[1], planes_of(1))
-        second_product(1)
+        quantise_z(1)
+        first_b1 = bank(0, 1, 128)
+        second_product(1, 0, first_b1[:, 0, :])
         interleave(nc.vector.tensor_copy, z[2], planes_of(2))
-        second_product(2)
-
-        own = keep.tile([P, PACK, S], F32, name="own")
-
-        def fill_window(t, b, copy):
-            c0, w = BLOCKS[b]
-            g = 0 if t < BANK_TILES[b][0][1] else 1
-            copy(h[t][:, c0 : c0 + w], h_ps[b, g][:, t - BANK_TILES[b][g][0], :])
-
-        def fill_own(b, g):
-            c0, w = BLOCKS[b]
-            t0, t1 = BANK_TILES[b][g]
-            nc.scalar.copy(own[:, t0:t1, c0 : c0 + w], h_ps[b, g][:])
+        quantise_z(2)
+        shared = bank(1, PACK, 128)
+        second_product(2, 0, shared[:, 0, :])
 
         fill_window(0, 0, nc.scalar.copy)
+        fill_own(0, 0, 1, h_ps[0, 0].unsqueeze(1))
         fill_window(0, 1, nc.scalar.copy)
-        fill_own(0, 0)
+        fill_own(1, 0, 1, first_b1[:])
         fill_window(0, 2, nc.vector.tensor_copy)
-        fill_own(1, 0)
-        fill_own(2, 0)
-        fill_own(2, 1)
+        fill_own(2, 0, 1, shared[:, 0:1, :])
+        rest_b2 = bank(2, PACK - 1, 128)
+        rest_b0 = bank(0, 2, HALF)
+        for t in range(1, PACK):
+            second_product(1, t, shared[:, t, :])
+        for t in range(1, PACK):
+            second_product(2, t, rest_b2[:, t - 1, :])
+        for t in (2, 3):
+            second_product(0, t, rest_b0[:, t - 2, :])
         for t in range(1, PACK):
             for b in range(len(BLOCKS)):
                 fill_window(t, b, nc.scalar.copy)
             if t == 1:
-                fill_own(0, 1)
+                fill_own(0, 1, 2, h_ps[0, 1].unsqueeze(1))
+                fill_own(1, 1, PACK, shared[:, 1:PACK, :])
+                fill_own(2, 1, PACK, rest_b2[:])
+                fill_own(0, 2, PACK, rest_b0[:])
 
         out_rows = out_0.rearrange("(p t) s -> p t s", t=PACK)
         out_words = words_of(out_1)
@@ -256,8 +260,8 @@ def tile_picked_laygatequad_none_po_kernel(
             cols = slice(c0, c0 + w)
             nc.vector.scalar_tensor_tensor(res[:, t, cols], d2[t][:, cols], 0.75, d3[t][:, cols], MULT, MULT)
 
-        def store(t, c0, w):
-            nc.sync.dma_start(out=out_rows[:, t, c0 : c0 + w], in_=res[:, t, c0 : c0 + w])
+        def store(t0, t1, c0, w):
+            nc.sync.dma_start(out=out_rows[:, t0:t1, c0 : c0 + w], in_=res[:, t0:t1, c0 : c0 + w])
 
         def regroup(copy, b):
             c0, w = BLOCKS[b]
@@ -270,27 +274,36 @@ def tile_picked_laygatequad_none_po_kernel(
         for c0 in (0, HALF):
             differ(d2, n2_t, 0, c0, HALF)
             differ(d3, n3_t, 0, c0, HALF)
-        for t in (1, 2):
-            differ(d2, n2_t, t, 0, S)
-            product(t - 1, 0, S)
-            store(t - 1, 0, S)
-            differ(d3, n3_t, t, 0, S)
-        for b, (c0, w) in enumerate(BLOCKS):
-            differ(d2, n2_t, 3, c0, w)
-            if b == 0:
-                product(2, 0, S)
-                store(2, 0, S)
-            else:
-                product(3, *BLOCKS[b - 1])
-                regroup(nc.scalar.copy, b - 1)
-            differ(d3, n3_t, 3, c0, w)
-        store(3, 0, HALF)
+        differ(d2, n2_t, 1, 0, S)
+        product(0, 0, S)
+        store(0, 1, 0, S)
+        differ(d3, n3_t, 1, 0, S)
+        differ(d2, n2_t, 2, 0, HALF)
+        product(1, 0, S)
+        store(1, 2, 0, S)
+        differ(d3, n3_t, 2, 0, HALF)
+        differ(d2, n2_t, 3, 0, HALF)
+        product(2, 0, HALF)
+        differ(d3, n3_t, 3, 0, HALF)
+        differ(d2, n2_t, 2, HALF, HALF)
+        product(3, 0, HALF)
+        store(2, PACK, 0, HALF)
+        regroup(nc.scalar.copy, 0)
+        differ(d3, n3_t, 2, HALF, HALF)
+        differ(d2, n2_t, 3, *BLOCKS[1])
+        product(2, HALF, HALF)
+        store(2, 3, HALF, HALF)
+        differ(d3, n3_t, 3, *BLOCKS[1])
         quantise(0)
         nc.sync.dma_start(out=out_words[:, halves[0]], in_=ow[:, halves[0]])
-        product(3, *BLOCKS[2])
-        store(3, HALF, HALF)
-        regroup(nc.vector.tensor_copy, 2)
+        product(3, *BLOCKS[1])
+        regroup(nc.scalar.copy, 1)
+        differ(d2, n2_t, 3, *BLOCKS[2])
+        differ(d3, n3_t, 3, *BLOCKS[2])
         quantise(1)
+        product(3, *BLOCKS[2])
+        store(3, PACK, HALF, HALF)
+        regroup(nc.vector.tensor_copy, 2)
         quantise(2)
         nc.sync.dma_start(out=out_words[:, halves[1]], in_=ow[:, halves[1]])
         for q in range(4):

from contextlib import ExitStack

import concourse.mybir as mybir

K, T, S, N, H = 512, 2048, 512, 512, 512
FLOPS = 2 * K * H * S + 2 * H * N * S

F32 = mybir.dt.float32
BF16 = mybir.dt.bfloat16
I32 = mybir.dt.int32
U32 = mybir.dt.uint32
U16 = mybir.dt.uint16
U8 = mybir.dt.uint8
FP8X4 = mybir.dt.float8_e4m3fn_x4
MULT = mybir.AluOpType.mult
SUB = mybir.AluOpType.subtract
SIGMOID = mybir.ActivationFunctionType.Sigmoid
COPY = mybir.ActivationFunctionType.Copy

P = 128
PACK = 4
LIST_ROWS = 16
HALF = S // 2
BLOCKS = ((0, 256), (256, 128), (384, 128))
W1_ROW = 4
W2_ROW = 8


def words_of(packed):
    return packed[0].rearrange("p n t -> p (n t)").bitcast(I32)


def entries(lists, start, width):
    return lists[:, start // LIST_ROWS : (start + width) // LIST_ROWS]


def load_scales(queues, plane, scales, row):
    for q in range(4):
        queues[q].dma_start(
            out=plane[32 * q + row : 32 * q + row + 4, :].bitcast(I32),
            in_=scales[0][4 * q : 4 * q + 4, :].bitcast(I32),
        )


def deal(nc, dealt, raw, run):
    nc.vector.tensor_copy(
        out=dealt[:].rearrange("p (t c i) -> p c t i", t=PACK, i=run),
        in_=raw[:].rearrange("p (c i t) -> p c t i", t=PACK, i=run),
    )


def interleave(copy, grouped, planes):
    copy(
        out=grouped[:].rearrange("p (c i t) -> p c t i", t=PACK, i=4),
        in_=planes.rearrange("p t (c i) -> p c t i", i=4),
    )


def tile_picked_laygatequad_none_po_kernel(
    tc, x_words, x_scales, w1_words, w1_scales, gn, w2_words, w2_scales, offs, n1, n2, n3, out_0, out_1, out_2
):
    nc = tc.nc
    with ExitStack() as ctx:
        lists = ctx.enter_context(tc.tile_pool(name="lists", bufs=1))
        keep = ctx.enter_context(tc.tile_pool(name="keep", bufs=1))
        psum = ctx.enter_context(tc.psum_pool(name="psum", bufs=1))

        offs_t = lists.tile([P, S // LIST_ROWS], U16, name="offs_t")
        n1_t = lists.tile([P, S // LIST_ROWS], U16, name="n1_t")
        n2_t = lists.tile([P, S // LIST_ROWS], U16, name="n2_t")
        n3_t = lists.tile([P, S // LIST_ROWS], U16, name="n3_t")

        xw = keep.tile([P, T], I32, name="xw", align_bytes=64)
        xs = keep.tile([P, T], U8, name="xs", tag="xs", align_bytes=64)
        w1w = keep.tile([P, H], I32, name="w1w", align_bytes=64)
        w1s = keep.tile([P, H], U8, name="w1s", align_bytes=64)
        w2w = keep.tile([P, N], I32, name="w2w", tag="w2w", align_bytes=64)
        w2s = keep.tile([P, N], U8, name="w2s", tag="w2s", align_bytes=64)
        gain = keep.tile([P, PACK], F32, name="gain")

        nc.gpsimd.memset(w1s[:].bitcast(I32), 0)
        nc.gpsimd.memset(xs[:].bitcast(I32)[:, 0:256], 0)
        nc.vector.memset(xs[:].bitcast(I32)[:, 256:512], 0)
        nc.vector.memset(w2s[:].bitcast(I32), 0)

        nc.sync.dma_start(offs_t[:], offs)
        nc.sync.dma_start(out=w1w[:], in_=words_of(w1_words))
        load_scales([nc.sync, nc.gpsimd, nc.gpsimd, nc.gpsimd], w1s, w1_scales, W1_ROW)
        load_scales([nc.sync] * 4, xs, x_scales, 0)
        nc.sync.dma_start(out=xw[:], in_=words_of(x_words))
        nc.sync.dma_start(out=gain[:], in_=gn.rearrange("(p t) o -> p (t o)", t=PACK))
        nc.sync.dma_start(n1_t[:], n1)
        nc.sync.dma_start(out=w2w[:], in_=words_of(w2_words))
        load_scales([nc.sync] * 4, w2s, w2_scales, W2_ROW)
        nc.sync.dma_start(n2_t[:], n2)
        nc.sync.dma_start(n3_t[:], n3)

        w1wd = keep.tile([P, H], I32, name="w1wd", align_bytes=64)
        deal(nc, w1wd, w1w, 4)
        xs_g = keep.tile([P, S], U8, name="xs_g", align_bytes=64)
        nc.vector.tensor_copy(xs_g[:], xs[:].indirect(offs_t[:]))
        w1sd = keep.tile([P, H], U8, name="w1sd", tag="xs", align_bytes=64)
        deal(nc, w1sd, w1s, 16)

        halves = [slice(0, HALF), slice(HALF, S)]
        xw_g = keep.tile([P, S], I32, name="xw_g", align_bytes=64)
        for half in range(2):
            nc.vector.tensor_copy(
                xw_g[:, halves[half]].bitcast(U32), xw[:].bitcast(U32).indirect(entries(offs_t, half * HALF, HALF))
            )

        def project(t, cols, tag):
            out = psum.tile([P, cols.stop - cols.start], F32, name=tag, tag=tag)
            nc.tensor.matmul_mx(
                out=out[:],
                lhsT=w1wd[:, t * P : (t + 1) * P].bitcast(FP8X4),
                lhsT_scale=w1sd[W1_ROW:P, t * P : (t + 1) * P],
                rhs=xw_g[:, cols].bitcast(FP8X4),
                rhs_scale=xs_g[:, cols],
                start=True,
                stop=True,
            )
            return out

        y_ps = {}
        for half in range(2):
            for t in (0, 1):
                y_ps[half, t] = project(t, halves[half], f"bank{2 * half + t}")
        for t in (2, 3):
            y_ps[t] = project(t, slice(0, S), f"bank{2 + t}")

        h = [keep.tile([P, 2 * S if t == 1 else S], F32, name=f"h{t}") for t in range(PACK)]
        y = [keep.tile([P, S], F32, name=f"y{t}") for t in range(PACK)]
        gate = {t: keep.tile([P, S], F32, name=f"gate{t}") for t in (2, 3)}

        w2sd = keep.tile([P, N], U8, name="w2sd", align_bytes=64)
        deal(nc, w2sd, w2s, 16)
        w2wd = keep.tile([P, N], I32, name="w2wd", tag="w2s", align_bytes=64)
        deal(nc, w2wd, w2w, 4)
        work = keep.tile([P, 2 * PACK + 2, HALF], F32, name="work", tag="w2w", align_bytes=64)
        z_planes = [work[:, PACK * half : PACK * (half + 1), :] for half in range(2)]
        scaled = [[work[:, 2 * PACK + half, :] for half in range(2)], [h[1][:, S : S + HALF], h[1][:, S + HALF : 2 * S]]]

        for half in range(2):
            for t in (0, 1):
                nc.scalar.activation(y[t][:, halves[half]], y_ps[half, t][:], SIGMOID)
        for half in range(2):
            nc.scalar.activation(scaled[1][half], y_ps[half, 1][:], COPY, scale=gain[:, 1:2])
        for t in (0, 1):
            for half in range(2):
                if t == 0:
                    nc.vector.tensor_scalar(scaled[0][half], y_ps[half, 0][:], gain[:, 0:1], None, MULT)
                nc.vector.tensor_tensor(
                    z_planes[half][:, t, :], y[t][:].indirect(entries(n1_t, half * HALF, HALF)), scaled[t][half], MULT
                )

        h_ps = {}
        z = [keep.tile([P, PACK * w], BF16, name=f"z{b}", align_bytes=64) for b, (c0, w) in enumerate(BLOCKS)]

        def planes_of(b):
            c0, w = BLOCKS[b]
            return z_planes[c0 // HALF][:, :, c0 % HALF : c0 % HALF + w]

        def gated(t, b):
            c0, w = BLOCKS[b]
            nc.scalar.activation(gate[t][:, c0 : c0 + w], y[t][:].indirect(entries(n1_t, c0, w)), SIGMOID)
            nc.vector.scalar_tensor_tensor(
                planes_of(b)[:, t, :], y[t][:, c0 : c0 + w], gain[:, t : t + 1], gate[t][:, c0 : c0 + w], MULT, MULT
            )

        zw = [keep.tile([P, w], I32, name=f"zw{b}", align_bytes=64) for b, (c0, w) in enumerate(BLOCKS)]
        zs = [keep.tile([P, w], U8, name=f"zs{b}", align_bytes=64) for b, (c0, w) in enumerate(BLOCKS)]

        def quantise_z(b):
            nc.vector.quantize_mx(out=zw[b][:].bitcast(FP8X4), scales=zs[b][:], in_=z[b][:])

        def second_product(b, t, out):
            h_ps[b, t] = out
            nc.tensor.matmul_mx(
                out=out,
                lhsT=w2wd[:, t * P : (t + 1) * P].bitcast(FP8X4),
                lhsT_scale=w2sd[W2_ROW:P, t * P : (t + 1) * P],
                rhs=zw[b][:].bitcast(FP8X4),
                rhs_scale=zs[b][:],
                start=True,
                stop=True,
            )

        def bank(number, tiles, width):
            return psum.tile([P, tiles, width], F32, name=f"bank{number}", tag=f"bank{number}")

        own = keep.tile([P, PACK, S], F32, name="own")

        def fill_window(t, b, copy):
            c0, w = BLOCKS[b]
            copy(h[t][:, c0 : c0 + w], h_ps[b, t])

        def fill_own(b, t0, t1, source):
            c0, w = BLOCKS[b]
            nc.scalar.copy(own[:, t0:t1, c0 : c0 + w], source)

        for t in (2, 3):
            nc.scalar.copy(y[t][:], y_ps[t][:])
            gated(t, 0)
        gated(2, 1)
        interleave(nc.vector.tensor_copy, z[0], planes_of(0))
        gated(3, 1)
        quantise_z(0)
        for t in (0, 1):
            second_product(0, t, bank(6 + t, 1, HALF)[:, 0, :])
        gated(2, 2)
        gated(3, 2)
        interleave(nc.scalar.copy, z[1], planes_of(1))
        quantise_z(1)
        first_b1 = bank(0, 1, 128)
        second_product(1, 0, first_b1[:, 0, :])
        interleave(nc.vector.tensor_copy, z[2], planes_of(2))
        quantise_z(2)
        shared = bank(1, PACK, 128)
        second_product(2, 0, shared[:, 0, :])

        fill_window(0, 0, nc.scalar.copy)
        fill_own(0, 0, 1, h_ps[0, 0].unsqueeze(1))
        fill_window(0, 1, nc.scalar.copy)
        fill_own(1, 0, 1, first_b1[:])
        fill_window(0, 2, nc.vector.tensor_copy)
        fill_own(2, 0, 1, shared[:, 0:1, :])
        rest_b2 = bank(2, PACK - 1, 128)
        rest_b0 = bank(0, 2, HALF)
        for t in range(1, PACK):
            second_product(1, t, shared[:, t, :])
        for t in range(1, PACK):
            second_product(2, t, rest_b2[:, t - 1, :])
        for t in (2, 3):
            second_product(0, t, rest_b0[:, t - 2, :])
        for t in range(1, PACK):
            for b in range(len(BLOCKS)):
                fill_window(t, b, nc.scalar.copy)
            if t == 1:
                fill_own(0, 1, 2, h_ps[0, 1].unsqueeze(1))
                fill_own(1, 1, PACK, shared[:, 1:PACK, :])
                fill_own(2, 1, PACK, rest_b2[:])
                fill_own(0, 2, PACK, rest_b0[:])

        out_rows = out_0.rearrange("(p t) s -> p t s", t=PACK)
        out_words = words_of(out_1)
        ow = keep.tile([P, S], I32, name="ow", align_bytes=64)
        osc = keep.tile([P, S], U8, name="osc", align_bytes=64)
        res = keep.tile([P, PACK, S], F32, name="res")
        d2 = [keep.tile([P, S], F32, name=f"d2_{t}") for t in range(PACK)]
        d3 = [keep.tile([P, S], F32, name=f"d3_{t}") for t in range(PACK)]
        grouped = [keep.tile([P, PACK * w], BF16, name=f"grouped{b}", align_bytes=64) for b, (c0, w) in enumerate(BLOCKS)]

        def differ(d, lists, t, c0, w):
            nc.vector.tensor_tensor(
                d[t][:, c0 : c0 + w], h[t][:].indirect(entries(lists, c0, w)), own[:, t, c0 : c0 + w], SUB
            )

        def product(t, c0, w):
            cols = slice(c0, c0 + w)
            nc.vector.scalar_tensor_tensor(res[:, t, cols], d2[t][:, cols], 0.75, d3[t][:, cols], MULT, MULT)

        def store(t0, t1, c0, w):
            nc.sync.dma_start(out=out_rows[:, t0:t1, c0 : c0 + w], in_=res[:, t0:t1, c0 : c0 + w])

        def regroup(copy, b):
            c0, w = BLOCKS[b]
            interleave(copy, grouped[b], res[:, :, c0 : c0 + w])

        def quantise(b):
            c0, w = BLOCKS[b]
            nc.vector.quantize_mx(out=ow[:, c0 : c0 + w].bitcast(FP8X4), scales=osc[:, c0 : c0 + w], in_=grouped[b][:])

        for c0 in (0, HALF):
            differ(d2, n2_t, 0, c0, HALF)
            differ(d3, n3_t, 0, c0, HALF)
        differ(d2, n2_t, 1, 0, S)
        product(0, 0, S)
        store(0, 1, 0, S)
        differ(d3, n3_t, 1, 0, S)
        differ(d2, n2_t, 2, 0, HALF)
        product(1, 0, S)
        store(1, 2, 0, S)
        differ(d3, n3_t, 2, 0, HALF)
        differ(d2, n2_t, 3, 0, HALF)
        product(2, 0, HALF)
        differ(d3, n3_t, 3, 0, HALF)
        differ(d2, n2_t, 2, HALF, HALF)
        product(3, 0, HALF)
        store(2, PACK, 0, HALF)
        regroup(nc.scalar.copy, 0)
        differ(d3, n3_t, 2, HALF, HALF)
        differ(d2, n2_t, 3, *BLOCKS[1])
        product(2, HALF, HALF)
        store(2, 3, HALF, HALF)
        differ(d3, n3_t, 3, *BLOCKS[1])
        quantise(0)
        nc.sync.dma_start(out=out_words[:, halves[0]], in_=ow[:, halves[0]])
        product(3, *BLOCKS[1])
        regroup(nc.scalar.copy, 1)
        differ(d2, n2_t, 3, *BLOCKS[2])
        differ(d3, n3_t, 3, *BLOCKS[2])
        quantise(1)
        product(3, *BLOCKS[2])
        store(3, PACK, HALF, HALF)
        regroup(nc.vector.tensor_copy, 2)
        quantise(2)
        nc.sync.dma_start(out=out_words[:, halves[1]], in_=ow[:, halves[1]])
        for q in range(4):
            queue = nc.sync if q % 2 else nc.scalar
            queue.dma_start(
                out=out_2[0][4 * q : 4 * q + 4, :].bitcast(I32), in_=osc[32 * q : 32 * q + 4, :].bitcast(I32)
            )
